import numpy as np
import ml_dtypes


def mxq(x, axis, fmt="e4m3"):
    dtype, down = {"e4m3": (ml_dtypes.float8_e4m3fn, 7), "e5m2": (ml_dtypes.float8_e5m2, 14)}[fmt]
    v = np.moveaxis(np.asarray(x, np.float32).astype(ml_dtypes.bfloat16).astype(np.float64), axis, -1)
    blocks = v.reshape(v.shape[:-1] + (-1, 32))
    amax = np.abs(blocks).max(-1, keepdims=True)
    byte = np.maximum(np.where(amax > 0, np.frexp(amax)[1] - 1 + 127, 0) - down, 1)
    scale = np.exp2(byte - 127.0)
    codes = (blocks / scale).astype(np.float32).astype(dtype).astype(np.float64)
    return np.moveaxis((codes * scale).reshape(v.shape), -1, axis)


WIDE = False


def mx_kscale(k):
    if not WIDE:
        return np.ones(k)
    levels = np.array([10, -10, 5, -5, 0])
    if k % 512:
        return np.exp2(np.random.permutation(np.resize(levels, k // 32))).repeat(32)
    a = np.empty((k // 512, 16))
    for p in range(k // 512):
        a[p, :8] = np.random.permutation(np.resize(levels, 8))
        for g in range(8):
            far = levels[np.abs(levels - a[p, g]) >= 10]
            a[p, g + 8] = far[np.random.randint(len(far))]
    return np.exp2(a.ravel()).repeat(32)


def f64(x):
    return np.asarray(x).astype(np.float64)


def striped(idx):
    return np.tile(idx.reshape(-1, 16).T, (8, 1)).astype(np.uint16)


def unstriped(offs):
    return offs[:16].T.reshape(-1).astype(np.int64)


E2M1 = np.array([0.0, 0.5, 1.0, 1.5, 2.0, 3.0, 4.0, 6.0, -0.0, -0.5, -1.0, -1.5, -2.0, -3.0, -4.0, -6.0])


def pack_weight(w, fmt):
    k, n = w.shape
    w = f64(np.asarray(w, np.float32).astype(ml_dtypes.bfloat16)).reshape(k // 32, 32, n)
    amax = np.abs(w).max(1)
    if fmt == "e4m3":
        byte = np.frexp(amax)[1] - 1 + 127 - 7
    else:
        mant, ex = np.frexp(amax / 6.0)
        byte = np.where(mant > 0.5, ex, ex - 1) + 127
    byte = np.clip(np.where(amax > 0, byte, 1), 1, 254)
    scaled = (w * np.exp2(127.0 - byte)[:, None, :]).reshape(k, n).astype(np.float32)
    by_word = np.ascontiguousarray(scaled.reshape(k // 512, 128, 4, n).transpose(0, 1, 3, 2))
    if fmt == "e4m3":
        words = by_word.astype(ml_dtypes.float8_e4m3fn).view(np.uint8)
    else:
        c = by_word.astype(ml_dtypes.float4_e2m1fn).view(np.uint8) & 0xF
        words = (c[..., 0::2] | (c[..., 1::2] << 4)).reshape(k // 512, 128, 2 * n)
    return np.ascontiguousarray(words), np.ascontiguousarray(byte.astype(np.uint8).reshape(k // 512, 16, n))


def unpack_weight(words, scales, fmt):
    g, _, n = scales.shape
    words = np.ascontiguousarray(words).reshape(g, 128, n, -1)
    if fmt == "e4m3":
        vals = words.view(ml_dtypes.float8_e4m3fn).astype(np.float64)
    else:
        nib = np.empty((g, 128, n, 4), np.uint8)
        nib[..., 0::2] = words & 0xF
        nib[..., 1::2] = words >> 4
        vals = E2M1[nib]
    vals = vals * np.repeat(np.exp2(scales.astype(np.float64) - 127.0), 8, axis=1)[..., None]
    return vals.transpose(0, 1, 3, 2).reshape(g * 512, n)


def gelu(v):
    return 0.5 * v * (1.0 + np.tanh(np.sqrt(2.0 / np.pi) * (v + 0.044715 * v**3)))


def striped8(idx):
    return np.concatenate([v.reshape(-1, 16).T for v in idx]).astype(np.uint16)


def unstriped8(offs):
    return np.stack([offs[16 * g:16 * g + 16].T.reshape(-1) for g in range(8)]).astype(np.int64)


def runs(v, idx8):
    k = np.arange(v.shape[0])
    return v[k[:, None], idx8[k % 512 // 64]]


def put_heads(h, wgs, idx8, t2):
    r = np.arange(h.shape[0])
    page = np.zeros((h.shape[0], t2))
    page[r[:, None], idx8[r % 512 // 64]] = wgs[r // 4 % 128] * h
    return page


K, T, S, T2 = 1024, 2048, 512, 1024

def setup_inputs():
    n = np.random.standard_normal
    s = mx_kscale(K)[:, None]
    tab_words, tab_scales = pack_weight(n((K, T)) * s, "e4m3")
    wa_words, wa_scales = pack_weight(n((K, K)) / np.sqrt(K) * s.T / s, "e2m1")
    return {
        "tab_words": tab_words, "tab_scales": tab_scales,
        "offs": striped8(np.stack([np.random.permutation(T)[:S] for _ in range(8)])),
        "wa_words": wa_words, "wa_scales": wa_scales,
        "wb": (n((K, K)) / np.sqrt(K) * s.T / s).astype(np.float32),
        "ca": (0.5 * n(K) * s[:, 0]).astype(np.float32),
        "cb": (0.5 * n(K) * s[:, 0]).astype(np.float32),
        "gain": (np.exp(0.3 * n(K)) / s[:, 0]).astype(np.float32),
        "wgo": np.repeat(np.random.uniform(0.5, 2.0, (8, S)), 16, axis=0).astype(np.float32),
        "offs2": striped8(np.stack([np.random.permutation(T2)[:S] for _ in range(8)])),
    }

def reference(tab_words, tab_scales, offs, wa_words, wa_scales, wb, ca, cb, gain, wgo, offs2):
    v = runs(unpack_weight(tab_words, tab_scales, "e4m3"), unstriped8(offs))
    A = unpack_weight(wa_words, wa_scales, "e2m1")
    B = mxq(f64(wb), 0, "e4m3")
    hb = (B.T @ v) + f64(cb)[:, None]
    ha = (A.T @ v) + f64(ca)[:, None]
    hbq = mxq(hb, 0, "e4m3")
    haq = mxq(ha, 0, "e4m3")
    ab = (A.T @ hbq) + f64(ca)[:, None]
    ba = (B.T @ haq) + f64(cb)[:, None]
    y = f64(gain)[:, None] * (ab - ba)
    return put_heads(y, f64(wgo), unstriped8(offs2), T2)

@@ -1,0 +1,284 @@
+from contextlib import ExitStack
+
+import concourse.mybir as mybir
+
+K, T, S, T2 = 1024, 2048, 512, 1024
+FLOPS = 4 * 2 * K * K * S
+
+F32 = mybir.dt.float32
+BF16 = mybir.dt.bfloat16
+I32 = mybir.dt.int32
+U32 = mybir.dt.uint32
+U16 = mybir.dt.uint16
+U8 = mybir.dt.uint8
+FP8X4 = mybir.dt.float8_e4m3fn_x4
+FP4X4 = mybir.dt.float4_e2m1fn_x4
+ALU = mybir.AluOpType
+IDENTITY = mybir.ActivationFunctionType.Identity
+
+P = 128
+PACK = 4
+K_PASS = P * PACK
+PASSES = K // K_PASS
+SCALE_ROWS = K_PASS // 32
+ROW_STEP = P // SCALE_ROWS
+BANK = 512
+CHUNK = 256
+HALF = 128
+PAGES = 5
+
+
+def tile_list_petal_order_commutator_kernel(
+    tc, tab_words, tab_scales, offs, wa_words, wa_scales, wb, ca, cb, gain, wgo, offs2, out
+):
+    nc = tc.nc
+    with ExitStack() as ctx:
+        lists = ctx.enter_context(tc.tile_pool(name="lists", bufs=1))
+        keep = ctx.enter_context(tc.tile_pool(name="keep", bufs=1))
+        stage = ctx.enter_context(tc.tile_pool(name="stage", bufs=1))
+        psum = ctx.enter_context(tc.psum_pool(name="psum", bufs=1))
+
+        def held(shape, dtype, name, tag=""):
+            return keep.tile(shape, dtype, name=name, tag=tag, align_bytes=64)
+
+        def bank(index, name):
+            return psum.tile([P, BANK], F32, name=name, tag="bank%d" % index)
+
+        pick = lists.tile([P, S // 16], U16, name="pick")
+        place = lists.tile([P, S // 16], U16, name="place")
+        nc.sync.dma_start(pick[:], offs)
+
+        wa_raw = held([P, PASSES * 2 * K], U8, "wa_raw")
+        nc.sync.dma_start(
+            out=wa_raw[:].bitcast(I32).rearrange("p (a c) -> p a c", a=PASSES),
+            in_=wa_words.bitcast(I32).rearrange("a p c -> p a c"),
+        )
+        tab_s = [held([P, T], U8, "tab_s%d" % a) for a in range(PASSES)]
+        for a in range(PASSES):
+            nc.vector.memset(tab_s[a][:].bitcast(I32), 0)
+            nc.sync.dma_start(out=tab_s[a][4:P:ROW_STEP, :].bitcast(I32), in_=tab_scales[a].bitcast(I32))
+        was_raw = stage.tile([P, PASSES * K], U8, name="was_raw", offset=0)
+        nc.vector.memset(was_raw[:].bitcast(I32), 0)
+        nc.sync.dma_start(
+            out=was_raw[4:P:ROW_STEP, :].bitcast(I32).rearrange("q (a c) -> q a c", a=PASSES),
+            in_=wa_scales.bitcast(I32).rearrange("a q c -> q a c"),
+        )
+
+        warm_in = stage.tile([P, 16], F32, name="warm_in", offset=32768)
+        warm_out = stage.tile([P, 16], F32, name="warm_out", offset=24576 - 32)
+        nc.vector.memset(warm_in[:], 0.0)
+        nc.scalar.activation(warm_out[:], warm_in[:], IDENTITY)
+
+        tab_w = [stage.tile([P, T], I32, name="tab_w%d" % a, offset=16384 + 8192 * a) for a in range(PASSES)]
+        for a in range(PASSES):
+            nc.sync.dma_start(out=tab_w[a][:], in_=tab_words[a].rearrange("p t i -> p (t i)").bitcast(I32))
+
+
+        def load_wb(a, first, width, name, offset):
+            raw = stage.tile([P, PACK, width], F32, name=name, offset=offset)
+            rows = wb[a * K_PASS : (a + 1) * K_PASS, first : first + width]
+            nc.sync.dma_start(out=raw[:], in_=rows.rearrange("(p j) c -> p j c", j=PACK))
+            return raw
+
+        wb_raw = {}
+        wb_raw[0, 0] = load_wb(0, 0, K_PASS, "wb_raw00", 32768)
+        nc.sync.dma_start(place[:], offs2)
+
+        vecs = {}
+        for name, vec in (("ca", ca), ("cb", cb), ("gain", gain)):
+            vecs[name] = held([P, PASSES, PACK], F32, name + "_sb")
+            nc.gpsimd.dma_start(out=vecs[name][:], in_=vec.rearrange("(b p t) -> p b t", p=P, t=PACK))
+
+
+        picked_s = stage.tile([P, PASSES * S], U8, name="picked_s", offset=2048)
+        for a in range(PASSES):
+            nc.vector.tensor_copy(picked_s[:, a * S : (a + 1) * S], tab_s[a][:].indirect(pick[:]))
+        planes = held([P, PASSES * S + PASSES * K], U8, "planes")
+        nc.vector.tensor_copy(planes[:, 0 : PASSES * S].bitcast(I32), picked_s[:].bitcast(I32))
+        nc.vector.tensor_copy(
+            planes[:, PASSES * S :].rearrange("p (g t m) -> p g m t", t=PACK, m=P),
+            was_raw[:].rearrange("p (g m t) -> p g m t", t=PACK, m=P),
+        )
+        for d in range(0, P, 32):
+            nc.sync.dma_start(
+                out=planes[d : d + 4, :].bitcast(I32), in_=planes[d + 4 : d + 32 : ROW_STEP, :].bitcast(I32)
+            )
+
+        wb_raw[1, 0] = load_wb(1, 0, K_PASS, "wb_raw10", 0)
+        v_w = [held([P, S], U32, "v_w%d" % a) for a in range(PASSES)]
+        for a in range(PASSES):
+            nc.vector.tensor_copy(v_w[a][:], tab_w[a][:].bitcast(U32).indirect(pick[:]))
+
+        wa_w = held([P, PASSES * 2 * K], U8, "wa_w")
+        nc.vector.tensor_copy(
+            wa_w[:].bitcast(U16).rearrange("p (g t m) -> p g m t", t=PACK, m=P),
+            wa_raw[:].bitcast(U16).rearrange("p (g m t) -> p g m t", t=PACK, m=P),
+        )
+
+        wb_raw[0, 1] = load_wb(0, K_PASS, K_PASS, "wb_raw01", 16384)
+        wb_last = [load_wb(1, K_PASS + u * CHUNK, CHUNK, "wb_last%d" % u, 24576 + 4096 * u) for u in range(2)]
+
+        neg_ca = held([P, PASSES, PACK], F32, "neg_ca")
+        nc.gpsimd.tensor_scalar(neg_ca[:], vecs["ca"][:], -1.0, 0.0, ALU.mult, ALU.add)
+        diff = held([P, PASSES, PACK], F32, "diff")
+        nc.gpsimd.tensor_tensor(diff[:], vecs["ca"][:], vecs["cb"][:], ALU.subtract)
+        y_bias = held([P, PASSES, PACK], F32, "y_bias")
+        nc.gpsimd.tensor_tensor(y_bias[:], diff[:], vecs["gain"][:], ALU.mult)
+
+        def a_side(a, b, t):
+            col = a * K + b * K_PASS + t * P
+            return wa_w[:, 2 * col : 2 * (col + P)].bitcast(FP4X4), planes[:, PASSES * S + col : PASSES * S + col + P]
+
+        wb_w, wb_s, wb_bf = {}, {}, {}
+
+        def b_side(a, b, t):
+            return wb_w[a, b][:, t * P : (t + 1) * P].bitcast(FP8X4), wb_s[a, b][:, t * P : (t + 1) * P]
+
+        def v_side(a, first, width):
+            return v_w[a][:, first : first + width].bitcast(FP8X4), planes[:, a * S + first : a * S + first + width]
+
+        def mx(dst, lhs, rhs, start, stop):
+            nc.tensor.matmul_mx(
+                out=dst, lhsT=lhs[0], lhsT_scale=lhs[1], rhs=rhs[0], rhs_scale=rhs[1], start=start, stop=stop
+            )
+
+        def cast_wb(copy, a, b, raw, m_raw, m_first, m_count):
+            dst = wb_bf[a, b][:].rearrange("p (t m j) -> p m j t", t=PACK, j=PACK)
+            src = raw[:].rearrange("p j (m t) -> p m j t", t=PACK)
+            copy(dst[:, m_first : m_first + m_count], src[:, m_raw : m_raw + m_count])
+
+        def quantize_wb(a, b):
+            wb_w[a, b] = held([P, K_PASS], U32, "wb_w%d%d" % (a, b))
+            wb_s[a, b] = held([P, K_PASS], U8, "wb_s%d%d" % (a, b))
+            nc.vector.quantize_mx(out=wb_w[a, b][:].bitcast(FP8X4), scales=wb_s[a, b][:], in_=wb_bf[a, b][:])
+
+        for a in range(PASSES):
+            for b in range(PASSES):
+                wb_bf[a, b] = held([P, K_PASS * PACK], BF16, "wb_bf%d%d" % (a, b))
+
+        h_w, h_s = {}, {}
+        for which in "ab":
+            for b in range(PASSES):
+                h_w[which, b] = held([P, S], U32, "h_w%s%d" % (which, b))
+                h_s[which, b] = held([P, S], U8, "h_s%s%d" % (which, b))
+
+        def h_side(which, b, first, width):
+            return h_w[which, b][:, first : first + width].bitcast(FP8X4), h_s[which, b][:, first : first + width]
+
+        def quantize_h(key, h_bf):
+            cols = slice(key[2] * CHUNK, (key[2] + 1) * CHUNK)
+            nc.vector.quantize_mx(out=h_w[key[:2]][:, cols].bitcast(FP8X4), scales=h_s[key[:2]][:, cols], in_=h_bf[:])
+
+        def stage1_vector(which, b, first_bank):
+            side = a_side if which == "a" else b_side
+            h_bf = held([P, CHUNK * PACK], BF16, "h_bf%s%d0" % (which, b))
+            accs = [bank(first_bank + u, "acc_%s%d0%d" % (which, b, u)) for u in range(2)]
+            for a in range(PASSES):
+                for u in range(2):
+                    for t in range(PACK):
+                        mx(
+                            accs[u][:, t * HALF : (t + 1) * HALF],
+                            side(a, b, t),
+                            v_side(a, u * HALF, HALF),
+                            a == 0 and t == 0,
+                            a == PASSES - 1 and t == PACK - 1,
+                        )
+            for u in range(2):
+                sums = accs[u][:].rearrange("p (t n) -> p n t", t=PACK)
+                dst = h_bf[:, u * HALF * PACK : (u + 1) * HALF * PACK].rearrange("p (n t) -> p n t", t=PACK)
+                if which == "a":
+                    bias = neg_ca[:, b, :].unsqueeze(1).to_broadcast([P, HALF, PACK])
+                    nc.vector.tensor_tensor(dst, bias, sums, ALU.subtract)
+                else:
+                    bias = vecs["cb"][:, b, :].unsqueeze(1).to_broadcast([P, HALF, PACK])
+                    nc.vector.tensor_tensor(dst, sums, bias, ALU.add)
+            quantize_h((which, b, 0), h_bf)
+
+        def stage1_scalar(which, b, first_bank):
+            rows = held([P, PACK, CHUNK], BF16, "h_rows%s%d" % (which, b))
+            h_bf = held([P, CHUNK * PACK], BF16, "h_bf%s%d1" % (which, b))
+            for u in range(2):
+                acc = bank(first_bank + u, "acc_%s%d1%d" % (which, b, u))
+                for t in range(2 * u, 2 * u + 2):
+                    col = (t - 2 * u) * CHUNK
+                    if which == "a":
+                        for w in range(2):
+                            for a in range(PASSES):
+                                mx(
+                                    acc[:, col + w * HALF : col + (w + 1) * HALF],
+                                    a_side(a, b, t),
+                                    v_side(a, CHUNK + w * HALF, HALF),
+                                    a == 0,
+                                    a == PASSES - 1,
+                                )
+                    else:
+                        for a in range(PASSES):
+                            mx(acc[:, col : col + CHUNK], b_side(a, b, t), v_side(a, CHUNK, CHUNK), a == 0, a == PASSES - 1)
+                for t in range(2 * u, 2 * u + 2):
+                    col = (t - 2 * u) * CHUNK
+                    if which == "a":
+                        nc.scalar.activation(
+                            rows[:, t, :], acc[:, col : col + CHUNK], IDENTITY, bias=neg_ca[:, b, t : t + 1], scale=-1.0
+                        )
+                    else:
+                        nc.scalar.activation(
+                            rows[:, t, :], acc[:, col : col + CHUNK], IDENTITY, bias=vecs["cb"][:, b, t : t + 1]
+                        )
+            nc.scalar.copy(h_bf[:].rearrange("p (n t) -> p n t", t=PACK), rows[:].rearrange("p t n -> p n t"))
+            quantize_h((which, b, 1), h_bf)
+
+        def stage2(i, first, width, bank_index):
+            b_out, t = divmod(i, PACK)
+            acc = bank(bank_index, "acc_y%d_%d" % (i, first))
+            for b in range(PASSES):
+                mx(acc[:, 0:width], b_side(b, b_out, t), h_side("a", b, first, width), b == 0, False)
+            step = width if width == S else HALF
+            for b in range(PASSES):
+                for w in range(0, width, step):
+                    last = b == PASSES - 1 and w + step == width
+                    mx(acc[:, w : w + step], a_side(b, b_out, t), h_side("b", b, first + w, step), False, last)
+            y = held([P, width], F32, "y%d_%d" % (i, first))
+            nc.scalar.activation(
+                y[:], acc[:, 0:width], IDENTITY, bias=y_bias[:, b_out, t : t + 1], scale=vecs["gain"][:, b_out, t : t + 1]
+            )
+            nc.vector.tensor_tensor(
+                pages[i % PAGES][:].indirect(place[:, first // 16 : (first + width) // 16]),
+                y[:],
+                wgo_sb[:, first : first + width],
+                ALU.mult,
+            )
+
+        cast_wb(nc.scalar.copy, 0, 0, wb_raw[0, 0], 0, 0, P)
+        quantize_wb(0, 0)
+        wgo_sb = stage.tile([P, S], F32, name="wgo_sb", offset=32768)
+        nc.sync.dma_start(out=wgo_sb[:], in_=wgo)
+        stage1_vector("a", 0, 0)
+        cast_wb(nc.scalar.copy, 1, 0, wb_raw[1, 0], 0, 0, P)
+        quantize_wb(1, 0)
+        stage1_vector("a", 1, 2)
+        cast_wb(nc.scalar.copy, 0, 1, wb_raw[0, 1], 0, 0, P)
+        stage1_vector("b", 0, 4)
+        quantize_wb(0, 1)
+        cast_wb(nc.vector.tensor_copy, 1, 1, wb_last[0], 0, 0, 64)
+        cast_wb(nc.vector.tensor_copy, 1, 1, wb_last[1], 0, 64, 40)
+        cast_wb(nc.scalar.copy, 1, 1, wb_last[1], 40, 104, 24)
+        quantize_wb(1, 1)
+        stage1_vector("b", 1, 6)
+        pages = [held([P, T2], F32, "page%d" % i) for i in range(PAGES)]
+        for page in pages:
+            nc.vector.memset(page[:], 0.0)
+        stage1_scalar("a", 0, 0)
+        stage1_scalar("a", 1, 2)
+        for i in range(4):
+            stage2(i, 0, CHUNK, 4 + i)
+        stage1_scalar("b", 0, 0)
+        stage1_scalar("b", 1, 2)
+        for i in range(4, PAGES):
+            stage2(i, 0, CHUNK, i - 4)
+        rows_out = out.rearrange("(b p t) c -> b t p c", p=P, t=PACK)
+        for i in range(8):
+            if i < PAGES:
+                stage2(i, CHUNK, CHUNK, (4 + i) % 8)
+            else:
+                stage2(i, 0, S, (4 + i) % 8)
+            nc.sync.dma_start(out=rows_out[i // PACK, i % PACK], in_=pages[i % PAGES][:])

@@ -48,11 +48,16 @@ def tile_list_petal_order_commutator_kernel(
         place = lists.tile([P, S // 16], U16, name="place")
         nc.sync.dma_start(pick[:], offs)
 
-        wa_raw = held([P, PASSES * 2 * K], U8, "wa_raw")
-        nc.sync.dma_start(
-            out=wa_raw[:].bitcast(I32).rearrange("p (a c) -> p a c", a=PASSES),
-            in_=wa_words.bitcast(I32).rearrange("a p c -> p a c"),
-        )
+        def load_wb(a, first, width, name, offset):
+            raw = stage.tile([P, PACK, width], F32, name=name, offset=offset)
+            rows = wb[a * K_PASS : (a + 1) * K_PASS, first : first + width]
+            nc.sync.dma_start(out=raw[:], in_=rows.rearrange("(p j) c -> p j c", j=PACK))
+            return raw
+
+        wb_raw = {}
+        wb_raw[0, 0] = load_wb(0, 0, K_PASS, "wb_raw00", 40960)
+        nc.sync.dma_start(place[:], offs2)
+
         tab_s = [held([P, T], U8, "tab_s%d" % a) for a in range(PASSES)]
         for a in range(PASSES):
             nc.vector.memset(tab_s[a][:].bitcast(I32), 0)
@@ -64,25 +69,20 @@ def tile_list_petal_order_commutator_kernel(
             in_=wa_scales.bitcast(I32).rearrange("a q c -> q a c"),
         )
 
-        warm_in = stage.tile([P, 16], F32, name="warm_in", offset=32768)
-        warm_out = stage.tile([P, 16], F32, name="warm_out", offset=24576 - 32)
+        warm_in = stage.tile([P, 16], F32, name="warm_in", offset=32768 - 32)
+        warm_out = stage.tile([P, 16], F32, name="warm_out", offset=16384 - 32)
         nc.vector.memset(warm_in[:], 0.0)
         nc.scalar.activation(warm_out[:], warm_in[:], IDENTITY)
 
-        tab_w = [stage.tile([P, T], I32, name="tab_w%d" % a, offset=16384 + 8192 * a) for a in range(PASSES)]
-        for a in range(PASSES):
+        wb_raw[1, 0] = load_wb(1, 0, K_PASS, "wb_raw10", 8192)
+        tab_w = [stage.tile([P, T], I32, name="tab_w%d" % a, offset=16384 + 16384 * a) for a in range(PASSES)]
+
+        def load_tab(a):
             nc.sync.dma_start(out=tab_w[a][:], in_=tab_words[a].rearrange("p t i -> p (t i)").bitcast(I32))
 
-
-        def load_wb(a, first, width, name, offset):
-            raw = stage.tile([P, PACK, width], F32, name=name, offset=offset)
-            rows = wb[a * K_PASS : (a + 1) * K_PASS, first : first + width]
-            nc.sync.dma_start(out=raw[:], in_=rows.rearrange("(p j) c -> p j c", j=PACK))
-            return raw
-
-        wb_raw = {}
-        wb_raw[0, 0] = load_wb(0, 0, K_PASS, "wb_raw00", 32768)
-        nc.sync.dma_start(place[:], offs2)
+        load_tab(0)
+        wb_raw[0, 1] = load_wb(0, K_PASS, K_PASS, "wb_raw01", 24576)
+        load_tab(1)
 
         vecs = {}
         for name, vec in (("ca", ca), ("cb", cb), ("gain", gain)):
@@ -104,7 +104,11 @@ def tile_list_petal_order_commutator_kernel(
                 out=planes[d : d + 4, :].bitcast(I32), in_=planes[d + 4 : d + 32 : ROW_STEP, :].bitcast(I32)
             )
 
-        wb_raw[1, 0] = load_wb(1, 0, K_PASS, "wb_raw10", 0)
+        wa_raw = stage.tile([P, PASSES * 2 * K], U8, name="wa_raw", offset=0)
+        nc.sync.dma_start(
+            out=wa_raw[:].bitcast(I32).rearrange("p (a c) -> p a c", a=PASSES),
+            in_=wa_words.bitcast(I32).rearrange("a p c -> p a c"),
+        )
         v_w = [held([P, S], U32, "v_w%d" % a) for a in range(PASSES)]
         for a in range(PASSES):
             nc.vector.tensor_copy(v_w[a][:], tab_w[a][:].bitcast(U32).indirect(pick[:]))
@@ -115,8 +119,6 @@ def tile_list_petal_order_commutator_kernel(
             wa_raw[:].bitcast(U16).rearrange("p (g m t) -> p g m t", t=PACK, m=P),
         )
 
-        wb_raw[0, 1] = load_wb(0, K_PASS, K_PASS, "wb_raw01", 16384)
-        wb_last = [load_wb(1, K_PASS + u * CHUNK, CHUNK, "wb_last%d" % u, 24576 + 4096 * u) for u in range(2)]
 
         neg_ca = held([P, PASSES, PACK], F32, "neg_ca")
         nc.gpsimd.tensor_scalar(neg_ca[:], vecs["ca"][:], -1.0, 0.0, ALU.mult, ALU.add)
@@ -171,7 +173,7 @@ def tile_list_petal_order_commutator_kernel(
 
         def stage1_vector(which, b, first_bank):
             side = a_side if which == "a" else b_side
-            h_bf = held([P, CHUNK * PACK], BF16, "h_bf%s%d0" % (which, b))
+            h_bf = held([P, CHUNK * PACK], BF16, "h_bf%s%d0" % (which, b), "h_bf%s%d0" % (which, b))
             accs = [bank(first_bank + u, "acc_%s%d0%d" % (which, b, u)) for u in range(2)]
             for a in range(PASSES):
                 for u in range(2):
@@ -194,36 +196,23 @@ def tile_list_petal_order_commutator_kernel(
                     nc.vector.tensor_tensor(dst, sums, bias, ALU.add)
             quantize_h((which, b, 0), h_bf)
 
-        def stage1_scalar(which, b, first_bank):
-            rows = held([P, PACK, CHUNK], BF16, "h_rows%s%d" % (which, b))
+        def multiply_for_scalar(which, b, first_bank):
+            accs = [bank(first_bank + u, "acc_%s%d1%d" % (which, b, u)) for u in range(2)]
+            side, step = (a_side, HALF) if which == "a" else (b_side, CHUNK)
+            sums = []
+            for t in range(PACK):
+                dst = accs[t // 2][:, (t % 2) * CHUNK : (t % 2 + 1) * CHUNK]
+                for w in range(0, CHUNK, step):
+                    for a in range(PASSES):
+                        mx(dst[:, w : w + step], side(a, b, t), v_side(a, CHUNK + w, step), a == 0, a == PASSES - 1)
+                sums.append(dst)
+            return sums
+
+        def finish_on_scalar(which, b, sums, rows):
             h_bf = held([P, CHUNK * PACK], BF16, "h_bf%s%d1" % (which, b))
-            for u in range(2):
-                acc = bank(first_bank + u, "acc_%s%d1%d" % (which, b, u))
-                for t in range(2 * u, 2 * u + 2):
-                    col = (t - 2 * u) * CHUNK
-                    if which == "a":
-                        for w in range(2):
-                            for a in range(PASSES):
-                                mx(
-                                    acc[:, col + w * HALF : col + (w + 1) * HALF],
-                                    a_side(a, b, t),
-                                    v_side(a, CHUNK + w * HALF, HALF),
-                                    a == 0,
-                                    a == PASSES - 1,
-                                )
-                    else:
-                        for a in range(PASSES):
-                            mx(acc[:, col : col + CHUNK], b_side(a, b, t), v_side(a, CHUNK, CHUNK), a == 0, a == PASSES - 1)
-                for t in range(2 * u, 2 * u + 2):
-                    col = (t - 2 * u) * CHUNK
-                    if which == "a":
-                        nc.scalar.activation(
-                            rows[:, t, :], acc[:, col : col + CHUNK], IDENTITY, bias=neg_ca[:, b, t : t + 1], scale=-1.0
-                        )
-                    else:
-                        nc.scalar.activation(
-                            rows[:, t, :], acc[:, col : col + CHUNK], IDENTITY, bias=vecs["cb"][:, b, t : t + 1]
-                        )
+            bias, scale = (neg_ca, -1.0) if which == "a" else (vecs["cb"], 1.0)
+            for t in range(PACK):
+                nc.scalar.activation(rows[:, t, :], sums[t], IDENTITY, bias=bias[:, b, t : t + 1], scale=scale)
             nc.scalar.copy(h_bf[:].rearrange("p (n t) -> p n t", t=PACK), rows[:].rearrange("p t n -> p n t"))
             quantize_h((which, b, 1), h_bf)
 
@@ -248,33 +237,37 @@ def tile_list_petal_order_commutator_kernel(
                 ALU.mult,
             )
 
-        cast_wb(nc.scalar.copy, 0, 0, wb_raw[0, 0], 0, 0, P)
-        quantize_wb(0, 0)
-        wgo_sb = stage.tile([P, S], F32, name="wgo_sb", offset=32768)
-        nc.sync.dma_start(out=wgo_sb[:], in_=wgo)
-        stage1_vector("a", 0, 0)
-        cast_wb(nc.scalar.copy, 1, 0, wb_raw[1, 0], 0, 0, P)
-        quantize_wb(1, 0)
-        stage1_vector("a", 1, 2)
+        for a in range(PASSES):
+            cast_wb(nc.scalar.copy, a, 0, wb_raw[a, 0], 0, 0, P)
+            quantize_wb(a, 0)
+        wb_last = [load_wb(1, K_PASS + u * CHUNK, CHUNK, "wb_last%d" % u, 8192 + 4096 * u) for u in range(2)]
         cast_wb(nc.scalar.copy, 0, 1, wb_raw[0, 1], 0, 0, P)
-        stage1_vector("b", 0, 4)
         quantize_wb(0, 1)
-        cast_wb(nc.vector.tensor_copy, 1, 1, wb_last[0], 0, 0, 64)
-        cast_wb(nc.vector.tensor_copy, 1, 1, wb_last[1], 0, 64, 40)
-        cast_wb(nc.scalar.copy, 1, 1, wb_last[1], 40, 104, 24)
+        wgo_sb = stage.tile([P, S], F32, name="wgo_sb", offset=24576)
+        nc.sync.dma_start(out=wgo_sb[:], in_=wgo)
+        stage1_vector("b", 0, 0)
+        for u in range(2):
+            cast_wb(nc.scalar.copy, 1, 1, wb_last[u], 0, 64 * u, 64)
         quantize_wb(1, 1)
+        stage1_vector("a", 0, 2)
+        stage1_vector("a", 1, 4)
         stage1_vector("b", 1, 6)
         pages = [held([P, T2], F32, "page%d" % i) for i in range(PAGES)]
         for page in pages:
-            nc.vector.memset(page[:], 0.0)
-        stage1_scalar("a", 0, 0)
-        stage1_scalar("a", 1, 2)
-        for i in range(4):
+            nc.vector.memset(page[:].bitcast(I32), 0)
+        for which, first_bank, offset in (("b", 0, 12288), ("a", 2, 14336)):
+            rows = stage.tile([P, PACK, CHUNK], BF16, name="rows_%s0" % which, offset=offset)
+            finish_on_scalar(which, 0, multiply_for_scalar(which, 0, first_bank), rows)
+        sums_a1 = multiply_for_scalar("a", 1, 0)
+        sums_b1 = multiply_for_scalar("b", 1, 2)
+        for i in range(0, 2):
             stage2(i, 0, CHUNK, 4 + i)
-        stage1_scalar("b", 0, 0)
-        stage1_scalar("b", 1, 2)
+        finish_on_scalar("a", 1, sums_a1, held([P, PACK, CHUNK], BF16, "rows_a1", "h_bfb10"))
+        for i in range(2, 4):
+            stage2(i, 0, CHUNK, 4 + i)
+        finish_on_scalar("b", 1, sums_b1, held([P, PACK, CHUNK], BF16, "rows_b1", "h_bfb10"))
         for i in range(4, PAGES):
-            stage2(i, 0, CHUNK, i - 4)
+            stage2(i, 0, CHUNK, i - 2)
         rows_out = out.rearrange("(b p t) c -> b t p c", p=P, t=PACK)
         for i in range(8):
             if i < PAGES:

@@ -1,6 +1,7 @@
 from contextlib import ExitStack
 
 import concourse.mybir as mybir
+from concourse.masks import make_identity
 
 K, T, S, T2 = 1024, 2048, 512, 1024
 FLOPS = 4 * 2 * K * K * S
@@ -20,12 +21,28 @@ P = 128
 PACK = 4
 K_PASS = P * PACK
 PASSES = K // K_PASS
-SCALE_ROWS = K_PASS // 32
-ROW_STEP = P // SCALE_ROWS
+TILES = K // P
+QUADRANT = 32
+LIST_ROWS = 16
 BANK = 512
 CHUNK = 256
-HALF = 128
+NARROW = 128
+
+ROW_STEP = 8
+ROW_FIRST = 4
+
 PAGES = 5
+
+KIB = 1024
+AT_TAB1 = 0
+AT_PICKED_SCALES = 2 * KIB
+AT_WA_SCALES = 7 * KIB
+AT_WB11 = 8 * KIB
+AT_TAB0 = 16 * KIB
+AT_WA_WORDS = 24 * KIB
+AT_WB0 = 28 * KIB
+AT_VECS = 32 * KIB
+AT_WB10 = 44 * KIB
 
 
 def tile_list_petal_order_commutator_kernel(
@@ -35,7 +52,7 @@ def tile_list_petal_order_commutator_kernel(
     with ExitStack() as ctx:
         lists = ctx.enter_context(tc.tile_pool(name="lists", bufs=1))
         keep = ctx.enter_context(tc.tile_pool(name="keep", bufs=1))
-        stage = ctx.enter_context(tc.tile_pool(name="stage", bufs=1))
+        loaded = ctx.enter_context(tc.tile_pool(name="loaded", bufs=1))
         psum = ctx.enter_context(tc.psum_pool(name="psum", bufs=1))
 
         def held(shape, dtype, name, tag=""):
@@ -44,234 +61,243 @@ def tile_list_petal_order_commutator_kernel(
         def bank(index, name):
             return psum.tile([P, BANK], F32, name=name, tag="bank%d" % index)
 
-        pick = lists.tile([P, S // 16], U16, name="pick")
-        place = lists.tile([P, S // 16], U16, name="place")
-        nc.sync.dma_start(pick[:], offs)
-
         def load_wb(a, first, width, name, offset):
-            raw = stage.tile([P, PACK, width], F32, name=name, offset=offset)
+            raw = loaded.tile([P, PACK, width], F32, name=name, offset=offset)
             rows = wb[a * K_PASS : (a + 1) * K_PASS, first : first + width]
             nc.sync.dma_start(out=raw[:], in_=rows.rearrange("(p j) c -> p j c", j=PACK))
             return raw
 
-        wb_raw = {}
-        wb_raw[0, 0] = load_wb(0, 0, K_PASS, "wb_raw00", 40960)
+        def load_tab(a, offset):
+            window = loaded.tile([P, T], I32, name="tab_w%d" % a, offset=offset)
+            nc.sync.dma_start(out=window[:], in_=tab_words[a].rearrange("p t i -> p (t i)").bitcast(I32))
+            return window
+
+        pick = lists.tile([P, S // LIST_ROWS], U16, name="pick")
+        place = lists.tile([P, S // LIST_ROWS], U16, name="place")
+        nc.sync.dma_start(pick[:], offs)
+        wb_raw10 = load_wb(1, 0, K_PASS, "wb_raw10", AT_WB10)
         nc.sync.dma_start(place[:], offs2)
 
         tab_s = [held([P, T], U8, "tab_s%d" % a) for a in range(PASSES)]
         for a in range(PASSES):
             nc.vector.memset(tab_s[a][:].bitcast(I32), 0)
-            nc.sync.dma_start(out=tab_s[a][4:P:ROW_STEP, :].bitcast(I32), in_=tab_scales[a].bitcast(I32))
-        was_raw = stage.tile([P, PASSES * K], U8, name="was_raw", offset=0)
-        nc.vector.memset(was_raw[:].bitcast(I32), 0)
+            nc.sync.dma_start(out=tab_s[a][ROW_FIRST:P:ROW_STEP, :].bitcast(I32), in_=tab_scales[a].bitcast(I32))
+        wa_s_raw = loaded.tile([P, PASSES * K], U8, name="wa_s_raw", offset=AT_WA_SCALES)
+        nc.vector.memset(wa_s_raw[:].bitcast(I32), 0)
         nc.sync.dma_start(
-            out=was_raw[4:P:ROW_STEP, :].bitcast(I32).rearrange("q (a c) -> q a c", a=PASSES),
+            out=wa_s_raw[ROW_FIRST:P:ROW_STEP, :].bitcast(I32).rearrange("q (a c) -> q a c", a=PASSES),
             in_=wa_scales.bitcast(I32).rearrange("a q c -> q a c"),
         )
 
-        warm_in = stage.tile([P, 16], F32, name="warm_in", offset=32768 - 32)
-        warm_out = stage.tile([P, 16], F32, name="warm_out", offset=16384 - 32)
+        warm_in = loaded.tile([P, 16], F32, name="warm_in", offset=AT_WB0)
+        warm_out = loaded.tile([P, 16], F32, name="warm_out", offset=AT_WA_WORDS - 32)
         nc.vector.memset(warm_in[:], 0.0)
         nc.scalar.activation(warm_out[:], warm_in[:], IDENTITY)
 
-        wb_raw[1, 0] = load_wb(1, 0, K_PASS, "wb_raw10", 8192)
-        tab_w = [stage.tile([P, T], I32, name="tab_w%d" % a, offset=16384 + 16384 * a) for a in range(PASSES)]
-
-        def load_tab(a):
-            nc.sync.dma_start(out=tab_w[a][:], in_=tab_words[a].rearrange("p t i -> p (t i)").bitcast(I32))
-
-        load_tab(0)
-        wb_raw[0, 1] = load_wb(0, K_PASS, K_PASS, "wb_raw01", 24576)
-        load_tab(1)
-
-        vecs = {}
-        for name, vec in (("ca", ca), ("cb", cb), ("gain", gain)):
-            vecs[name] = held([P, PASSES, PACK], F32, name + "_sb")
-            nc.gpsimd.dma_start(out=vecs[name][:], in_=vec.rearrange("(b p t) -> p b t", p=P, t=PACK))
-
-
-        picked_s = stage.tile([P, PASSES * S], U8, name="picked_s", offset=2048)
-        for a in range(PASSES):
-            nc.vector.tensor_copy(picked_s[:, a * S : (a + 1) * S], tab_s[a][:].indirect(pick[:]))
-        planes = held([P, PASSES * S + PASSES * K], U8, "planes")
-        nc.vector.tensor_copy(planes[:, 0 : PASSES * S].bitcast(I32), picked_s[:].bitcast(I32))
-        nc.vector.tensor_copy(
-            planes[:, PASSES * S :].rearrange("p (g t m) -> p g m t", t=PACK, m=P),
-            was_raw[:].rearrange("p (g m t) -> p g m t", t=PACK, m=P),
-        )
-        for d in range(0, P, 32):
-            nc.sync.dma_start(
-                out=planes[d : d + 4, :].bitcast(I32), in_=planes[d + 4 : d + 32 : ROW_STEP, :].bitcast(I32)
-            )
-
-        wa_raw = stage.tile([P, PASSES * 2 * K], U8, name="wa_raw", offset=0)
+        wb_raw0 = load_wb(0, 0, K, "wb_raw0", AT_WB0)
+        tab_w = [load_tab(0, AT_TAB0)]
+        wa_w_raw = loaded.tile([P, PASSES * 2 * K], U8, name="wa_w_raw", offset=AT_WA_WORDS)
         nc.sync.dma_start(
-            out=wa_raw[:].bitcast(I32).rearrange("p (a c) -> p a c", a=PASSES),
+            out=wa_w_raw[:].bitcast(I32).rearrange("p (a c) -> p a c", a=PASSES),
             in_=wa_words.bitcast(I32).rearrange("a p c -> p a c"),
         )
+
+        vec_rows = held([P, K_PASS], F32, "vec_rows")
+        nc.vector.memset(vec_rows[:], 0.0)
+        for index, vec in enumerate((ca, cb, gain)):
+            rows = vec_rows[index * PASSES : (index + 1) * PASSES, :]
+            nc.gpsimd.dma_start(out=rows, in_=vec.rearrange("(b c) -> b c", b=PASSES))
+        identity = held([P, P], F32, "identity")
+        make_identity(nc, identity[:])
+        turned = bank(7, "turned")
+        for t in range(PACK):
+            nc.tensor.transpose(turned[:, t * P : (t + 1) * P], vec_rows[:, t:K_PASS:PACK], identity[:])
+
+        picked_s = loaded.tile([P, PASSES * S], U8, name="picked_s", offset=AT_PICKED_SCALES)
+        for a in range(PASSES):
+            nc.vector.tensor_copy(picked_s[:, a * S : (a + 1) * S], tab_s[a][:].indirect(pick[:]))
+        scales = held([P, PASSES * S + PASSES * K], U8, "scales")
+        nc.vector.tensor_copy(scales[:, 0 : PASSES * S].bitcast(I32), picked_s[:].bitcast(I32))
+        nc.vector.tensor_copy(
+            scales[:, PASSES * S :].rearrange("p (g t m) -> p g t m", t=PACK, m=P),
+            wa_s_raw[:].rearrange("p (g m t) -> p g t m", t=PACK, m=P),
+        )
+        for d in range(0, P, QUADRANT):
+            nc.sync.dma_start(
+                out=scales[d : d + QUADRANT // ROW_STEP, :].bitcast(I32),
+                in_=scales[d + ROW_FIRST : d + QUADRANT : ROW_STEP, :].bitcast(I32),
+            )
+        tab_w.append(load_tab(1, AT_TAB1))
+        wb_raw11 = load_wb(1, K_PASS, K_PASS, "wb_raw11", AT_WB11)
+
         v_w = [held([P, S], U32, "v_w%d" % a) for a in range(PASSES)]
         for a in range(PASSES):
             nc.vector.tensor_copy(v_w[a][:], tab_w[a][:].bitcast(U32).indirect(pick[:]))
 
         wa_w = held([P, PASSES * 2 * K], U8, "wa_w")
         nc.vector.tensor_copy(
-            wa_w[:].bitcast(U16).rearrange("p (g t m) -> p g m t", t=PACK, m=P),
-            wa_raw[:].bitcast(U16).rearrange("p (g m t) -> p g m t", t=PACK, m=P),
+            wa_w[:].bitcast(U16).rearrange("p (g t m) -> p g t m", t=PACK, m=P),
+            wa_w_raw[:].bitcast(U16).rearrange("p (g m t) -> p g t m", t=PACK, m=P),
         )
 
-
-        neg_ca = held([P, PASSES, PACK], F32, "neg_ca")
-        nc.gpsimd.tensor_scalar(neg_ca[:], vecs["ca"][:], -1.0, 0.0, ALU.mult, ALU.add)
-        diff = held([P, PASSES, PACK], F32, "diff")
-        nc.gpsimd.tensor_tensor(diff[:], vecs["ca"][:], vecs["cb"][:], ALU.subtract)
-        y_bias = held([P, PASSES, PACK], F32, "y_bias")
-        nc.gpsimd.tensor_tensor(y_bias[:], diff[:], vecs["gain"][:], ALU.mult)
-
-        def a_side(a, b, t):
-            col = a * K + b * K_PASS + t * P
-            return wa_w[:, 2 * col : 2 * (col + P)].bitcast(FP4X4), planes[:, PASSES * S + col : PASSES * S + col + P]
-
-        wb_w, wb_s, wb_bf = {}, {}, {}
-
-        def b_side(a, b, t):
-            return wb_w[a, b][:, t * P : (t + 1) * P].bitcast(FP8X4), wb_s[a, b][:, t * P : (t + 1) * P]
-
-        def v_side(a, first, width):
-            return v_w[a][:, first : first + width].bitcast(FP8X4), planes[:, a * S + first : a * S + first + width]
-
-        def mx(dst, lhs, rhs, start, stop):
-            nc.tensor.matmul_mx(
-                out=dst, lhsT=lhs[0], lhsT_scale=lhs[1], rhs=rhs[0], rhs_scale=rhs[1], start=start, stop=stop
-            )
-
-        def cast_wb(copy, a, b, raw, m_raw, m_first, m_count):
-            dst = wb_bf[a, b][:].rearrange("p (t m j) -> p m j t", t=PACK, j=PACK)
-            src = raw[:].rearrange("p j (m t) -> p m j t", t=PACK)
-            copy(dst[:, m_first : m_first + m_count], src[:, m_raw : m_raw + m_count])
-
-        def quantize_wb(a, b):
-            wb_w[a, b] = held([P, K_PASS], U32, "wb_w%d%d" % (a, b))
-            wb_s[a, b] = held([P, K_PASS], U8, "wb_s%d%d" % (a, b))
-            nc.vector.quantize_mx(out=wb_w[a, b][:].bitcast(FP8X4), scales=wb_s[a, b][:], in_=wb_bf[a, b][:])
-
-        for a in range(PASSES):
-            for b in range(PASSES):
-                wb_bf[a, b] = held([P, K_PASS * PACK], BF16, "wb_bf%d%d" % (a, b))
-
-        h_w, h_s = {}, {}
+        wb_w, wb_s, h_w, h_s = {}, {}, {}, {}
         for which in "ab":
             for b in range(PASSES):
                 h_w[which, b] = held([P, S], U32, "h_w%s%d" % (which, b))
                 h_s[which, b] = held([P, S], U8, "h_s%s%d" % (which, b))
 
+        def wa_side(a, b, t):
+            col = a * K + b * K_PASS + t * P
+            return wa_w[:, 2 * col : 2 * (col + P)].bitcast(FP4X4), scales[:, PASSES * S + col : PASSES * S + col + P]
+
+        def wb_side(a, b, t):
+            return wb_w[a, b][:, t * P : (t + 1) * P].bitcast(FP8X4), wb_s[a, b][:, t * P : (t + 1) * P]
+
+        def v_side(a, first, width):
+            return v_w[a][:, first : first + width].bitcast(FP8X4), scales[:, a * S + first : a * S + first + width]
+
         def h_side(which, b, first, width):
             return h_w[which, b][:, first : first + width].bitcast(FP8X4), h_s[which, b][:, first : first + width]
 
-        def quantize_h(key, h_bf):
-            cols = slice(key[2] * CHUNK, (key[2] + 1) * CHUNK)
-            nc.vector.quantize_mx(out=h_w[key[:2]][:, cols].bitcast(FP8X4), scales=h_s[key[:2]][:, cols], in_=h_bf[:])
+        def multiply(dst, stationary, moving, start, stop):
+            nc.tensor.matmul_mx(
+                out=dst,
+                lhsT=stationary[0],
+                lhsT_scale=stationary[1],
+                rhs=moving[0],
+                rhs_scale=moving[1],
+                start=start,
+                stop=stop,
+            )
 
-        def stage1_vector(which, b, first_bank):
-            side = a_side if which == "a" else b_side
-            h_bf = held([P, CHUNK * PACK], BF16, "h_bf%s%d0" % (which, b), "h_bf%s%d0" % (which, b))
-            accs = [bank(first_bank + u, "acc_%s%d0%d" % (which, b, u)) for u in range(2)]
+        def quantize_wb(a, b, raw):
+            rounded = held([P, K_PASS * PACK], BF16, "wb_bf%d%d" % (a, b))
+            nc.scalar.copy(
+                rounded[:].rearrange("p (t m j) -> p m j t", t=PACK, j=PACK),
+                raw.rearrange("p j (m t) -> p m j t", t=PACK),
+            )
+            wb_w[a, b] = held([P, K_PASS], U32, "wb_w%d%d" % (a, b))
+            wb_s[a, b] = held([P, K_PASS], U8, "wb_s%d%d" % (a, b))
+            nc.vector.quantize_mx(out=wb_w[a, b][:].bitcast(FP8X4), scales=wb_s[a, b][:], in_=rounded[:])
+
+        def quantize_h(which, b, chunk, rounded):
+            words, scale_bytes = h_side(which, b, chunk * CHUNK, CHUNK)
+            nc.vector.quantize_mx(out=words, scales=scale_bytes, in_=rounded[:])
+
+        def first_stage_on_vector(which, b, first_bank):
+            side = wa_side if which == "a" else wb_side
+            rounded = held([P, CHUNK * PACK], BF16, "h_bf%s%d0" % (which, b), "h_bf%s%d0" % (which, b))
+            accs = [bank(first_bank + u, "acc_%s%d0%d" % (which, b, u)) for u in range(CHUNK // NARROW)]
             for a in range(PASSES):
-                for u in range(2):
+                for u, acc in enumerate(accs):
                     for t in range(PACK):
-                        mx(
-                            accs[u][:, t * HALF : (t + 1) * HALF],
-                            side(a, b, t),
-                            v_side(a, u * HALF, HALF),
-                            a == 0 and t == 0,
-                            a == PASSES - 1 and t == PACK - 1,
-                        )
-            for u in range(2):
-                sums = accs[u][:].rearrange("p (t n) -> p n t", t=PACK)
-                dst = h_bf[:, u * HALF * PACK : (u + 1) * HALF * PACK].rearrange("p (n t) -> p n t", t=PACK)
+                        start = a == 0 and t == 0
+                        stop = a == PASSES - 1 and t == PACK - 1
+                        dst = acc[:, t * NARROW : (t + 1) * NARROW]
+                        multiply(dst, side(a, b, t), v_side(a, u * NARROW, NARROW), start, stop)
+            for u, acc in enumerate(accs):
+                sums = acc[:].rearrange("p (t n) -> p n t", t=PACK)
+                dst = rounded[:, u * BANK : (u + 1) * BANK].rearrange("p (n t) -> p n t", t=PACK)
                 if which == "a":
-                    bias = neg_ca[:, b, :].unsqueeze(1).to_broadcast([P, HALF, PACK])
+                    bias = neg_ca[:, b, :].unsqueeze(1).to_broadcast([P, NARROW, PACK])
                     nc.vector.tensor_tensor(dst, bias, sums, ALU.subtract)
                 else:
-                    bias = vecs["cb"][:, b, :].unsqueeze(1).to_broadcast([P, HALF, PACK])
+                    bias = cb_sb[:, b, :].unsqueeze(1).to_broadcast([P, NARROW, PACK])
                     nc.vector.tensor_tensor(dst, sums, bias, ALU.add)
-            quantize_h((which, b, 0), h_bf)
+            quantize_h(which, b, 0, rounded)
 
         def multiply_for_scalar(which, b, first_bank):
-            accs = [bank(first_bank + u, "acc_%s%d1%d" % (which, b, u)) for u in range(2)]
-            side, step = (a_side, HALF) if which == "a" else (b_side, CHUNK)
+            side, step = (wa_side, NARROW) if which == "a" else (wb_side, CHUNK)
             sums = []
-            for t in range(PACK):
-                dst = accs[t // 2][:, (t % 2) * CHUNK : (t % 2 + 1) * CHUNK]
-                for w in range(0, CHUNK, step):
-                    for a in range(PASSES):
-                        mx(dst[:, w : w + step], side(a, b, t), v_side(a, CHUNK + w, step), a == 0, a == PASSES - 1)
-                sums.append(dst)
+            for u in range(PACK * CHUNK // BANK):
+                acc = bank(first_bank + u, "acc_%s%d1%d" % (which, b, u))
+                for a in range(PASSES):
+                    for col in range(0, BANK, step):
+                        t, entry = divmod(u * BANK + col, CHUNK)
+                        start = a == 0 and col == 0
+                        stop = a == PASSES - 1 and col + step == BANK
+                        multiply(acc[:, col : col + step], side(a, b, t), v_side(a, CHUNK + entry, step), start, stop)
+                sums.extend([acc[:, 0:CHUNK], acc[:, CHUNK:BANK]])
             return sums
 
-        def finish_on_scalar(which, b, sums, rows):
-            h_bf = held([P, CHUNK * PACK], BF16, "h_bf%s%d1" % (which, b))
-            bias, scale = (neg_ca, -1.0) if which == "a" else (vecs["cb"], 1.0)
+        def round_on_scalar(which, b, sums, rows):
+            bias, scale = (neg_ca, -1.0) if which == "a" else (cb_sb, 1.0)
             for t in range(PACK):
                 nc.scalar.activation(rows[:, t, :], sums[t], IDENTITY, bias=bias[:, b, t : t + 1], scale=scale)
-            nc.scalar.copy(h_bf[:].rearrange("p (n t) -> p n t", t=PACK), rows[:].rearrange("p t n -> p n t"))
-            quantize_h((which, b, 1), h_bf)
 
-        def stage2(i, first, width, bank_index):
-            b_out, t = divmod(i, PACK)
-            acc = bank(bank_index, "acc_y%d_%d" % (i, first))
+        def interleave_on_scalar(which, b, rows):
+            rounded = held([P, CHUNK * PACK], BF16, "h_bf%s%d1" % (which, b))
+            nc.scalar.copy(rounded[:].rearrange("p (n t) -> p n t", t=PACK), rows[:].rearrange("p t n -> p n t"))
+            quantize_h(which, b, 1, rounded)
+
+        def second_stage(tile_index, first, width, bank_index):
+            b_out, t = divmod(tile_index, PACK)
+            acc = bank(bank_index, "acc_y%d_%d" % (tile_index, first))
             for b in range(PASSES):
-                mx(acc[:, 0:width], b_side(b, b_out, t), h_side("a", b, first, width), b == 0, False)
-            step = width if width == S else HALF
+                multiply(acc[:, 0:width], wb_side(b, b_out, t), h_side("a", b, first, width), b == 0, False)
+            step = width if width == S else NARROW
             for b in range(PASSES):
-                for w in range(0, width, step):
-                    last = b == PASSES - 1 and w + step == width
-                    mx(acc[:, w : w + step], a_side(b, b_out, t), h_side("b", b, first + w, step), False, last)
-            y = held([P, width], F32, "y%d_%d" % (i, first))
+                for col in range(0, width, step):
+                    stop = b == PASSES - 1 and col + step == width
+                    moving = h_side("b", b, first + col, step)
+                    multiply(acc[:, col : col + step], wa_side(b, b_out, t), moving, False, stop)
+            y = held([P, width], F32, "y%d_%d" % (tile_index, first))
             nc.scalar.activation(
-                y[:], acc[:, 0:width], IDENTITY, bias=y_bias[:, b_out, t : t + 1], scale=vecs["gain"][:, b_out, t : t + 1]
+                y[:], acc[:, 0:width], IDENTITY, bias=y_bias[:, b_out, t : t + 1], scale=gain_sb[:, b_out, t : t + 1]
             )
             nc.vector.tensor_tensor(
-                pages[i % PAGES][:].indirect(place[:, first // 16 : (first + width) // 16]),
+                pages[tile_index % PAGES][:].indirect(place[:, first // LIST_ROWS : (first + width) // LIST_ROWS]),
                 y[:],
                 wgo_sb[:, first : first + width],
                 ALU.mult,
             )
 
-        for a in range(PASSES):
-            cast_wb(nc.scalar.copy, a, 0, wb_raw[a, 0], 0, 0, P)
-            quantize_wb(a, 0)
-        wb_last = [load_wb(1, K_PASS + u * CHUNK, CHUNK, "wb_last%d" % u, 8192 + 4096 * u) for u in range(2)]
-        cast_wb(nc.scalar.copy, 0, 1, wb_raw[0, 1], 0, 0, P)
-        quantize_wb(0, 1)
-        wgo_sb = stage.tile([P, S], F32, name="wgo_sb", offset=24576)
+        quantize_wb(1, 0, wb_raw10[:])
+        for b in range(PASSES):
+            quantize_wb(0, b, wb_raw0[:, :, b * K_PASS : (b + 1) * K_PASS])
+        wgo_sb = loaded.tile([P, S], F32, name="wgo_sb", offset=AT_WB0)
         nc.sync.dma_start(out=wgo_sb[:], in_=wgo)
-        stage1_vector("b", 0, 0)
-        for u in range(2):
-            cast_wb(nc.scalar.copy, 1, 1, wb_last[u], 0, 64 * u, 64)
-        quantize_wb(1, 1)
-        stage1_vector("a", 0, 2)
-        stage1_vector("a", 1, 4)
-        stage1_vector("b", 1, 6)
-        pages = [held([P, T2], F32, "page%d" % i) for i in range(PAGES)]
+
+        vecs = loaded.tile([P, 3 * PASSES, PACK], F32, name="vecs", offset=AT_VECS)
+        nc.scalar.copy(vecs[:], turned[:].rearrange("p (t row) -> p row t", t=PACK)[:, 0 : 3 * PASSES, :])
+        ca_sb, cb_sb, gain_sb = [vecs[:, index * PASSES : (index + 1) * PASSES, :] for index in range(3)]
+        neg_ca = held([P, PASSES, PACK], F32, "neg_ca")
+        nc.gpsimd.tensor_scalar(neg_ca[:], ca_sb, -1.0, 0.0, ALU.mult, ALU.add)
+        ca_less_cb = held([P, PASSES, PACK], F32, "ca_less_cb")
+        nc.gpsimd.tensor_tensor(ca_less_cb[:], ca_sb, cb_sb, ALU.subtract)
+        y_bias = held([P, PASSES, PACK], F32, "y_bias")
+        nc.gpsimd.tensor_tensor(y_bias[:], ca_less_cb[:], gain_sb, ALU.mult)
+
+        first_stage_on_vector("b", 0, 0)
+        quantize_wb(1, 1, wb_raw11[:])
+        first_stage_on_vector("a", 0, 2)
+        first_stage_on_vector("a", 1, 4)
+        first_stage_on_vector("b", 1, 6)
+        pages = [held([P, T2], F32, "page%d" % index) for index in range(PAGES)]
         for page in pages:
             nc.vector.memset(page[:].bitcast(I32), 0)
-        for which, first_bank, offset in (("b", 0, 12288), ("a", 2, 14336)):
-            rows = stage.tile([P, PACK, CHUNK], BF16, name="rows_%s0" % which, offset=offset)
-            finish_on_scalar(which, 0, multiply_for_scalar(which, 0, first_bank), rows)
+
+        rows_bytes = PACK * CHUNK * 2
+        for index, which in enumerate("ba"):
+            rows = loaded.tile([P, PACK, CHUNK], BF16, name="rows_%s0" % which, offset=AT_WB11 + index * rows_bytes)
+            round_on_scalar(which, 0, multiply_for_scalar(which, 0, 2 * index), rows)
+            interleave_on_scalar(which, 0, rows)
+
         sums_a1 = multiply_for_scalar("a", 1, 0)
+        second_stage(0, 0, CHUNK, 4)
         sums_b1 = multiply_for_scalar("b", 1, 2)
-        for i in range(0, 2):
-            stage2(i, 0, CHUNK, 4 + i)
-        finish_on_scalar("a", 1, sums_a1, held([P, PACK, CHUNK], BF16, "rows_a1", "h_bfb10"))
-        for i in range(2, 4):
-            stage2(i, 0, CHUNK, 4 + i)
-        finish_on_scalar("b", 1, sums_b1, held([P, PACK, CHUNK], BF16, "rows_b1", "h_bfb10"))
-        for i in range(4, PAGES):
-            stage2(i, 0, CHUNK, i - 2)
+        for index, (which, sums) in enumerate((("a", sums_a1), ("b", sums_b1))):
+            rows = held([P, PACK, CHUNK], BF16, "rows_%s1" % which, "h_bfb10")
+            round_on_scalar(which, 1, sums, rows)
+            second_stage(2 * index + 1, 0, CHUNK, 2 * index + 5)
+            interleave_on_scalar(which, 1, rows)
+            second_stage(2 * index + 2, 0, CHUNK, (2 * index + 6) % TILES)
+
         rows_out = out.rearrange("(b p t) c -> b t p c", p=P, t=PACK)
-        for i in range(8):
-            if i < PAGES:
-                stage2(i, CHUNK, CHUNK, (4 + i) % 8)
+        for tile_index in range(TILES):
+            bank_index = (1 + tile_index) % TILES
+            if tile_index < PAGES:
+                second_stage(tile_index, CHUNK, CHUNK, bank_index)
             else:
-                stage2(i, 0, S, (4 + i) % 8)
-            nc.sync.dma_start(out=rows_out[i // PACK, i % PACK], in_=pages[i % PAGES][:])
+                second_stage(tile_index, 0, S, bank_index)
+            nc.sync.dma_start(out=rows_out[tile_index // PACK, tile_index % PACK], in_=pages[tile_index % PAGES][:])

@@ -81,18 +81,13 @@ def tile_list_petal_order_commutator_kernel(
         tab_s = [held([P, T], U8, "tab_s%d" % a) for a in range(PASSES)]
         for a in range(PASSES):
             nc.vector.memset(tab_s[a][:].bitcast(I32), 0)
-            nc.sync.dma_start(out=tab_s[a][ROW_FIRST:P:ROW_STEP, :].bitcast(I32), in_=tab_scales[a].bitcast(I32))
+            nc.scalar.dma_start(out=tab_s[a][ROW_FIRST:P:ROW_STEP, :].bitcast(I32), in_=tab_scales[a].bitcast(I32))
         wa_s_raw = loaded.tile([P, PASSES * K], U8, name="wa_s_raw", offset=AT_WA_SCALES)
         nc.vector.memset(wa_s_raw[:].bitcast(I32), 0)
-        nc.sync.dma_start(
+        nc.scalar.dma_start(
             out=wa_s_raw[ROW_FIRST:P:ROW_STEP, :].bitcast(I32).rearrange("q (a c) -> q a c", a=PASSES),
             in_=wa_scales.bitcast(I32).rearrange("a q c -> q a c"),
         )
-
-        warm_in = loaded.tile([P, 16], F32, name="warm_in", offset=AT_WB0)
-        warm_out = loaded.tile([P, 16], F32, name="warm_out", offset=AT_WA_WORDS - 32)
-        nc.vector.memset(warm_in[:], 0.0)
-        nc.scalar.activation(warm_out[:], warm_in[:], IDENTITY)
 
         wb_raw0 = load_wb(0, 0, K, "wb_raw0", AT_WB0)
         tab_w = [load_tab(0, AT_TAB0)]

from contextlib import ExitStack

import concourse.mybir as mybir
from concourse.masks import make_identity

K, T, S, T2 = 1024, 2048, 512, 1024
FLOPS = 4 * 2 * K * K * S

F32 = mybir.dt.float32
BF16 = mybir.dt.bfloat16
I32 = mybir.dt.int32
U32 = mybir.dt.uint32
U16 = mybir.dt.uint16
U8 = mybir.dt.uint8
FP8X4 = mybir.dt.float8_e4m3fn_x4
FP4X4 = mybir.dt.float4_e2m1fn_x4
ALU = mybir.AluOpType
IDENTITY = mybir.ActivationFunctionType.Identity

P = 128
PACK = 4
K_PASS = P * PACK
PASSES = K // K_PASS
TILES = K // P
QUADRANT = 32
LIST_ROWS = 16
BANK = 512
CHUNK = 256
NARROW = 128

ROW_STEP = 8
ROW_FIRST = 4

PAGES = 5

KIB = 1024
AT_TAB1 = 0
AT_PICKED_SCALES = 2 * KIB
AT_WA_SCALES = 7 * KIB
AT_WB11 = 8 * KIB
AT_TAB0 = 16 * KIB
AT_WA_WORDS = 24 * KIB
AT_WB0 = 28 * KIB
AT_VECS = 32 * KIB
AT_WB10 = 44 * KIB


def tile_list_petal_order_commutator_kernel(
    tc, tab_words, tab_scales, offs, wa_words, wa_scales, wb, ca, cb, gain, wgo, offs2, out
):
    nc = tc.nc
    with ExitStack() as ctx:
        lists = ctx.enter_context(tc.tile_pool(name="lists", bufs=1))
        keep = ctx.enter_context(tc.tile_pool(name="keep", bufs=1))
        loaded = ctx.enter_context(tc.tile_pool(name="loaded", bufs=1))
        psum = ctx.enter_context(tc.psum_pool(name="psum", bufs=1))

        def held(shape, dtype, name, tag=""):
            return keep.tile(shape, dtype, name=name, tag=tag, align_bytes=64)

        def bank(index, name):
            return psum.tile([P, BANK], F32, name=name, tag="bank%d" % index)

        def load_wb(a, first, width, name, offset):
            raw = loaded.tile([P, PACK, width], F32, name=name, offset=offset)
            rows = wb[a * K_PASS : (a + 1) * K_PASS, first : first + width]
            nc.sync.dma_start(out=raw[:], in_=rows.rearrange("(p j) c -> p j c", j=PACK))
            return raw

        def load_tab(a, offset):
            window = loaded.tile([P, T], I32, name="tab_w%d" % a, offset=offset)
            nc.sync.dma_start(out=window[:], in_=tab_words[a].rearrange("p t i -> p (t i)").bitcast(I32))
            return window

        pick = lists.tile([P, S // LIST_ROWS], U16, name="pick")
        place = lists.tile([P, S // LIST_ROWS], U16, name="place")
        nc.sync.dma_start(pick[:], offs)
        wb_raw10 = load_wb(1, 0, K_PASS, "wb_raw10", AT_WB10)
        nc.sync.dma_start(place[:], offs2)

        tab_s = [held([P, T], U8, "tab_s%d" % a) for a in range(PASSES)]
        for a in range(PASSES):
            nc.vector.memset(tab_s[a][:].bitcast(I32), 0)
            nc.scalar.dma_start(out=tab_s[a][ROW_FIRST:P:ROW_STEP, :].bitcast(I32), in_=tab_scales[a].bitcast(I32))
        wa_s_raw = loaded.tile([P, PASSES * K], U8, name="wa_s_raw", offset=AT_WA_SCALES)
        nc.vector.memset(wa_s_raw[:].bitcast(I32), 0)
        nc.scalar.dma_start(
            out=wa_s_raw[ROW_FIRST:P:ROW_STEP, :].bitcast(I32).rearrange("q (a c) -> q a c", a=PASSES),
            in_=wa_scales.bitcast(I32).rearrange("a q c -> q a c"),
        )

        wb_raw0 = load_wb(0, 0, K, "wb_raw0", AT_WB0)
        tab_w = [load_tab(0, AT_TAB0)]
        wa_w_raw = loaded.tile([P, PASSES * 2 * K], U8, name="wa_w_raw", offset=AT_WA_WORDS)
        nc.sync.dma_start(
            out=wa_w_raw[:].bitcast(I32).rearrange("p (a c) -> p a c", a=PASSES),
            in_=wa_words.bitcast(I32).rearrange("a p c -> p a c"),
        )

        vec_rows = held([P, K_PASS], F32, "vec_rows")
        nc.vector.memset(vec_rows[:], 0.0)
        for index, vec in enumerate((ca, cb, gain)):
            rows = vec_rows[index * PASSES : (index + 1) * PASSES, :]
            nc.gpsimd.dma_start(out=rows, in_=vec.rearrange("(b c) -> b c", b=PASSES))
        identity = held([P, P], F32, "identity")
        make_identity(nc, identity[:])
        turned = bank(7, "turned")
        for t in range(PACK):
            nc.tensor.transpose(turned[:, t * P : (t + 1) * P], vec_rows[:, t:K_PASS:PACK], identity[:])

        picked_s = loaded.tile([P, PASSES * S], U8, name="picked_s", offset=AT_PICKED_SCALES)
        for a in range(PASSES):
            nc.vector.tensor_copy(picked_s[:, a * S : (a + 1) * S], tab_s[a][:].indirect(pick[:]))
        scales = held([P, PASSES * S + PASSES * K], U8, "scales")
        nc.vector.tensor_copy(scales[:, 0 : PASSES * S].bitcast(I32), picked_s[:].bitcast(I32))
        nc.vector.tensor_copy(
            scales[:, PASSES * S :].rearrange("p (g t m) -> p g t m", t=PACK, m=P),
            wa_s_raw[:].rearrange("p (g m t) -> p g t m", t=PACK, m=P),
        )
        for d in range(0, P, QUADRANT):
            nc.sync.dma_start(
                out=scales[d : d + QUADRANT // ROW_STEP, :].bitcast(I32),
                in_=scales[d + ROW_FIRST : d + QUADRANT : ROW_STEP, :].bitcast(I32),
            )
        tab_w.append(load_tab(1, AT_TAB1))
        wb_raw11 = load_wb(1, K_PASS, K_PASS, "wb_raw11", AT_WB11)

        v_w = [held([P, S], U32, "v_w%d" % a) for a in range(PASSES)]
        for a in range(PASSES):
            nc.vector.tensor_copy(v_w[a][:], tab_w[a][:].bitcast(U32).indirect(pick[:]))

        wa_w = held([P, PASSES * 2 * K], U8, "wa_w")
        nc.vector.tensor_copy(
            wa_w[:].bitcast(U16).rearrange("p (g t m) -> p g t m", t=PACK, m=P),
            wa_w_raw[:].bitcast(U16).rearrange("p (g m t) -> p g t m", t=PACK, m=P),
        )

        wb_w, wb_s, h_w, h_s = {}, {}, {}, {}
        for which in "ab":
            for b in range(PASSES):
                h_w[which, b] = held([P, S], U32, "h_w%s%d" % (which, b))
                h_s[which, b] = held([P, S], U8, "h_s%s%d" % (which, b))

        def wa_side(a, b, t):
            col = a * K + b * K_PASS + t * P
            return wa_w[:, 2 * col : 2 * (col + P)].bitcast(FP4X4), scales[:, PASSES * S + col : PASSES * S + col + P]

        def wb_side(a, b, t):
            return wb_w[a, b][:, t * P : (t + 1) * P].bitcast(FP8X4), wb_s[a, b][:, t * P : (t + 1) * P]

        def v_side(a, first, width):
            return v_w[a][:, first : first + width].bitcast(FP8X4), scales[:, a * S + first : a * S + first + width]

        def h_side(which, b, first, width):
            return h_w[which, b][:, first : first + width].bitcast(FP8X4), h_s[which, b][:, first : first + width]

        def multiply(dst, stationary, moving, start, stop):
            nc.tensor.matmul_mx(
                out=dst,
                lhsT=stationary[0],
                lhsT_scale=stationary[1],
                rhs=moving[0],
                rhs_scale=moving[1],
                start=start,
                stop=stop,
            )

        def quantize_wb(a, b, raw):
            rounded = held([P, K_PASS * PACK], BF16, "wb_bf%d%d" % (a, b))
            nc.scalar.copy(
                rounded[:].rearrange("p (t m j) -> p m j t", t=PACK, j=PACK),
                raw.rearrange("p j (m t) -> p m j t", t=PACK),
            )
            wb_w[a, b] = held([P, K_PASS], U32, "wb_w%d%d" % (a, b))
            wb_s[a, b] = held([P, K_PASS], U8, "wb_s%d%d" % (a, b))
            nc.vector.quantize_mx(out=wb_w[a, b][:].bitcast(FP8X4), scales=wb_s[a, b][:], in_=rounded[:])

        def quantize_h(which, b, chunk, rounded):
            words, scale_bytes = h_side(which, b, chunk * CHUNK, CHUNK)
            nc.vector.quantize_mx(out=words, scales=scale_bytes, in_=rounded[:])

        def first_stage_on_vector(which, b, first_bank):
            side = wa_side if which == "a" else wb_side
            rounded = held([P, CHUNK * PACK], BF16, "h_bf%s%d0" % (which, b), "h_bf%s%d0" % (which, b))
            accs = [bank(first_bank + u, "acc_%s%d0%d" % (which, b, u)) for u in range(CHUNK // NARROW)]
            for a in range(PASSES):
                for u, acc in enumerate(accs):
                    for t in range(PACK):
                        start = a == 0 and t == 0
                        stop = a == PASSES - 1 and t == PACK - 1
                        dst = acc[:, t * NARROW : (t + 1) * NARROW]
                        multiply(dst, side(a, b, t), v_side(a, u * NARROW, NARROW), start, stop)
            for u, acc in enumerate(accs):
                sums = acc[:].rearrange("p (t n) -> p n t", t=PACK)
                dst = rounded[:, u * BANK : (u + 1) * BANK].rearrange("p (n t) -> p n t", t=PACK)
                if which == "a":
                    bias = neg_ca[:, b, :].unsqueeze(1).to_broadcast([P, NARROW, PACK])
                    nc.vector.tensor_tensor(dst, bias, sums, ALU.subtract)
                else:
                    bias = cb_sb[:, b, :].unsqueeze(1).to_broadcast([P, NARROW, PACK])
                    nc.vector.tensor_tensor(dst, sums, bias, ALU.add)
            quantize_h(which, b, 0, rounded)

        def multiply_for_scalar(which, b, first_bank):
            side, step = (wa_side, NARROW) if which == "a" else (wb_side, CHUNK)
            sums = []
            for u in range(PACK * CHUNK // BANK):
                acc = bank(first_bank + u, "acc_%s%d1%d" % (which, b, u))
                for a in range(PASSES):
                    for col in range(0, BANK, step):
                        t, entry = divmod(u * BANK + col, CHUNK)
                        start = a == 0 and col == 0
                        stop = a == PASSES - 1 and col + step == BANK
                        multiply(acc[:, col : col + step], side(a, b, t), v_side(a, CHUNK + entry, step), start, stop)
                sums.extend([acc[:, 0:CHUNK], acc[:, CHUNK:BANK]])
            return sums

        def round_on_scalar(which, b, sums, rows):
            bias, scale = (neg_ca, -1.0) if which == "a" else (cb_sb, 1.0)
            for t in range(PACK):
                nc.scalar.activation(rows[:, t, :], sums[t], IDENTITY, bias=bias[:, b, t : t + 1], scale=scale)

        def interleave_on_scalar(which, b, rows):
            rounded = held([P, CHUNK * PACK], BF16, "h_bf%s%d1" % (which, b))
            nc.scalar.copy(rounded[:].rearrange("p (n t) -> p n t", t=PACK), rows[:].rearrange("p t n -> p n t"))
            quantize_h(which, b, 1, rounded)

        def second_stage(tile_index, first, width, bank_index):
            b_out, t = divmod(tile_index, PACK)
            acc = bank(bank_index, "acc_y%d_%d" % (tile_index, first))
            for b in range(PASSES):
                multiply(acc[:, 0:width], wb_side(b, b_out, t), h_side("a", b, first, width), b == 0, False)
            step = width if width == S else NARROW
            for b in range(PASSES):
                for col in range(0, width, step):
                    stop = b == PASSES - 1 and col + step == width
                    moving = h_side("b", b, first + col, step)
                    multiply(acc[:, col : col + step], wa_side(b, b_out, t), moving, False, stop)
            y = held([P, width], F32, "y%d_%d" % (tile_index, first))
            nc.scalar.activation(
                y[:], acc[:, 0:width], IDENTITY, bias=y_bias[:, b_out, t : t + 1], scale=gain_sb[:, b_out, t : t + 1]
            )
            nc.vector.tensor_tensor(
                pages[tile_index % PAGES][:].indirect(place[:, first // LIST_ROWS : (first + width) // LIST_ROWS]),
                y[:],
                wgo_sb[:, first : first + width],
                ALU.mult,
            )

        quantize_wb(1, 0, wb_raw10[:])
        for b in range(PASSES):
            quantize_wb(0, b, wb_raw0[:, :, b * K_PASS : (b + 1) * K_PASS])
        wgo_sb = loaded.tile([P, S], F32, name="wgo_sb", offset=AT_WB0)
        nc.sync.dma_start(out=wgo_sb[:], in_=wgo)

        vecs = loaded.tile([P, 3 * PASSES, PACK], F32, name="vecs", offset=AT_VECS)
        nc.scalar.copy(vecs[:], turned[:].rearrange("p (t row) -> p row t", t=PACK)[:, 0 : 3 * PASSES, :])
        ca_sb, cb_sb, gain_sb = [vecs[:, index * PASSES : (index + 1) * PASSES, :] for index in range(3)]
        neg_ca = held([P, PASSES, PACK], F32, "neg_ca")
        nc.gpsimd.tensor_scalar(neg_ca[:], ca_sb, -1.0, 0.0, ALU.mult, ALU.add)
        ca_less_cb = held([P, PASSES, PACK], F32, "ca_less_cb")
        nc.gpsimd.tensor_tensor(ca_less_cb[:], ca_sb, cb_sb, ALU.subtract)
        y_bias = held([P, PASSES, PACK], F32, "y_bias")
        nc.gpsimd.tensor_tensor(y_bias[:], ca_less_cb[:], gain_sb, ALU.mult)

        first_stage_on_vector("b", 0, 0)
        quantize_wb(1, 1, wb_raw11[:])
        first_stage_on_vector("a", 0, 2)
        first_stage_on_vector("a", 1, 4)
        first_stage_on_vector("b", 1, 6)
        pages = [held([P, T2], F32, "page%d" % index) for index in range(PAGES)]
        for page in pages:
            nc.vector.memset(page[:].bitcast(I32), 0)

        rows_bytes = PACK * CHUNK * 2
        for index, which in enumerate("ba"):
            rows = loaded.tile([P, PACK, CHUNK], BF16, name="rows_%s0" % which, offset=AT_WB11 + index * rows_bytes)
            round_on_scalar(which, 0, multiply_for_scalar(which, 0, 2 * index), rows)
            interleave_on_scalar(which, 0, rows)

        sums_a1 = multiply_for_scalar("a", 1, 0)
        second_stage(0, 0, CHUNK, 4)
        sums_b1 = multiply_for_scalar("b", 1, 2)
        for index, (which, sums) in enumerate((("a", sums_a1), ("b", sums_b1))):
            rows = held([P, PACK, CHUNK], BF16, "rows_%s1" % which, "h_bfb10")
            round_on_scalar(which, 1, sums, rows)
            second_stage(2 * index + 1, 0, CHUNK, 2 * index + 5)
            interleave_on_scalar(which, 1, rows)
            second_stage(2 * index + 2, 0, CHUNK, (2 * index + 6) % TILES)

        rows_out = out.rearrange("(b p t) c -> b t p c", p=P, t=PACK)
        for tile_index in range(TILES):
            bank_index = (1 + tile_index) % TILES
            if tile_index < PAGES:
                second_stage(tile_index, CHUNK, CHUNK, bank_index)
            else:
                second_stage(tile_index, 0, S, bank_index)
            nc.sync.dma_start(out=rows_out[tile_index // PACK, tile_index % PACK], in_=pages[tile_index % PAGES][:])
